import numpy as np
import ml_dtypes


def mxq(x, axis, fmt="e4m3"):
    dtype, down = {"e4m3": (ml_dtypes.float8_e4m3fn, 7), "e5m2": (ml_dtypes.float8_e5m2, 14)}[fmt]
    v = np.moveaxis(np.asarray(x, np.float32).astype(ml_dtypes.bfloat16).astype(np.float64), axis, -1)
    blocks = v.reshape(v.shape[:-1] + (-1, 32))
    amax = np.abs(blocks).max(-1, keepdims=True)
    byte = np.maximum(np.where(amax > 0, np.frexp(amax)[1] - 1 + 127, 0) - down, 1)
    scale = np.exp2(byte - 127.0)
    codes = (blocks / scale).astype(np.float32).astype(dtype).astype(np.float64)
    return np.moveaxis((codes * scale).reshape(v.shape), -1, axis)


WIDE = False


def mx_kscale(k):
    if not WIDE:
        return np.ones(k)
    levels = np.array([10, -10, 5, -5, 0])
    if k % 512:
        return np.exp2(np.random.permutation(np.resize(levels, k // 32))).repeat(32)
    a = np.empty((k // 512, 16))
    for p in range(k // 512):
        a[p, :8] = np.random.permutation(np.resize(levels, 8))
        for g in range(8):
            far = levels[np.abs(levels - a[p, g]) >= 10]
            a[p, g + 8] = far[np.random.randint(len(far))]
    return np.exp2(a.ravel()).repeat(32)


def f64(x):
    return np.asarray(x).astype(np.float64)


def striped(idx):
    return np.tile(idx.reshape(-1, 16).T, (8, 1)).astype(np.uint16)


def unstriped(offs):
    return offs[:16].T.reshape(-1).astype(np.int64)


def pack_weight(w):
    k, n = w.shape
    w = f64(np.asarray(w, np.float32).astype(ml_dtypes.bfloat16)).reshape(k // 32, 32, n)
    amax = np.abs(w).max(1)
    byte = np.clip(np.where(amax > 0, np.frexp(amax)[1] - 1 + 127 - 7, 1), 1, 254)
    scaled = (w * np.exp2(127.0 - byte)[:, None, :]).reshape(k, n).astype(np.float32)
    words = np.ascontiguousarray(scaled.reshape(k // 512, 128, 4, n).transpose(0, 1, 3, 2)).astype(ml_dtypes.float8_e4m3fn).view(np.uint8)
    return words, np.ascontiguousarray(byte.astype(np.uint8).reshape(k // 512, 16, n))


def unpack_weight(words, scales):
    g, p, n, _ = words.shape
    vals = np.ascontiguousarray(words).view(ml_dtypes.float8_e4m3fn).astype(np.float64) * np.repeat(np.exp2(scales.astype(np.float64) - 127.0), 8, axis=1)[..., None]
    return vals.transpose(0, 1, 3, 2).reshape(g * 512, n)


def planes(y):
    n, m = y.shape
    v = y.astype(np.float32).astype(ml_dtypes.bfloat16).astype(np.float64).reshape(n // 32, 32, m)
    top = np.abs(v).max(1)
    byte = np.clip(np.where(top > 0, np.frexp(top)[1] - 1 + 127 - 7, 1), 1, 254)
    codes = (v * np.exp2(127.0 - byte)[:, None, :]).reshape(n, m).astype(np.float32).astype(ml_dtypes.float8_e4m3fn).view(np.uint8)
    words = codes.reshape(n // 512, 128, 4, m).transpose(0, 1, 3, 2)
    return np.ascontiguousarray(words), np.ascontiguousarray(byte.astype(np.uint8).reshape(n // 512, 16, m))


K, T, S, N, H, W = 512, 1024, 512, 512, 512, 1024


def setup_inputs():
    n = np.random.standard_normal
    s = mx_kscale(K)[:, None]
    u = mx_kscale(H)
    packed_xT = pack_weight(n((K, T)) * s)
    packed_eT = pack_weight(n((K, W)) * s)
    return {
        "x_words": packed_xT[0],
        "x_scales": packed_xT[1],
        "w1": (n((K, N)) / np.sqrt(K) / s).astype(np.float32),
        "e_words": packed_eT[0],
        "e_scales": packed_eT[1],
        "w2": (n((K, N)) / np.sqrt(K) / s).astype(np.float32),
        "unit": (np.random.uniform(0.6, 1.4, (H, 1)) * u[:, None]).astype(np.float32),
        "w3": (n((H, N)) / np.sqrt(H) / u[:, None]).astype(np.float32),
        "offs": striped(np.random.permutation(T)[:S]),
        "mds": striped(np.random.permutation(W)[:S]),
        "md": striped(np.random.permutation(S)),
        "prv": striped(np.random.permutation(S)),
    }


def reference(x_words, x_scales, w1, e_words, e_scales, w2, unit, w3, offs, mds, md, prv):
    xq = unpack_weight(x_words, x_scales)[:, unstriped(offs)]
    y = mxq(f64(w1), 0, "e4m3").T @ xq
    e_mds = unpack_weight(e_words, e_scales)[:, unstriped(mds)]
    ye = mxq(f64(w2), 0, "e4m3").T @ e_mds
    em = ye[:, unstriped(md)]
    res1 = y + em
    rp = res1[:, unstriped(prv)]
    hid = f64(unit) * (np.maximum(rp, em) - res1)
    out_0 = mxq(f64(w3), 0, "e4m3").T @ mxq(hid, 0, "e4m3")
    return (out_0,) + planes(out_0)

@@ -1,0 +1,233 @@
+from contextlib import ExitStack
+
+import concourse.mybir as mybir
+
+K, T, S, N = 512, 1024, 512, 512
+FLOPS = 3 * 2 * 512 * 512 * 512
+
+F32 = mybir.dt.float32
+BF16 = mybir.dt.bfloat16
+I32 = mybir.dt.int32
+U32 = mybir.dt.uint32
+U16 = mybir.dt.uint16
+U8 = mybir.dt.uint8
+FP8X4 = mybir.dt.float8_e4m3fn_x4
+ALU = mybir.AluOpType
+COPY = mybir.ActivationFunctionType.Copy
+
+P = 128
+PACK = 4
+HALF = 256
+CHUNKS = ((0, 256), (256, 384), (384, 512))
+
+
+def tile_picked_ytransc_max_po_kernel(
+    tc, x_words, x_scales, w1, e_words, e_scales, w2, unit, w3, offs, mds, md, prv, out_0, out_1, out_2
+):
+    nc = tc.nc
+    with ExitStack() as ctx:
+        lists = ctx.enter_context(tc.tile_pool(name="lists", bufs=1))
+        keep = ctx.enter_context(tc.tile_pool(name="keep", bufs=1))
+        psum = ctx.enter_context(tc.psum_pool(name="psum", bufs=1))
+
+        def sb(shape, dtype, name):
+            return keep.tile(shape, dtype, name=name, align_bytes=64)
+
+        def load_list(src, name):
+            tile = lists.tile([P, S // 16], U16, name=name)
+            nc.sync.dma_start(tile[:], src)
+            return tile
+
+        def scale_table(name):
+            tile = sb([P, T], U8, name)
+            nc.gpsimd.memset(tile[:].bitcast(I32), 0)
+            return tile
+
+        def load_scale_rows(queue, tile, src, quadrants):
+            for q in quadrants:
+                queue.dma_start(tile[32 * q : 32 * q + 4, :].bitcast(I32), src[0, 4 * q : 4 * q + 4, :].bitcast(I32))
+
+        def load_word_table(src, name):
+            tile = sb([P, T], I32, name)
+            nc.sync.dma_start(tile[:], src[0].rearrange("p n t -> p (n t)").bitcast(I32))
+            return tile
+
+        def load_weight_half(w, h, name):
+            tile = sb([P, PACK, HALF], F32, name)
+            nc.sync.dma_start(tile[:], w.rearrange("(p j) c -> p j c", j=PACK)[:, :, h * HALF : (h + 1) * HALF])
+            return tile
+
+        def deal(copy, grouped, raw, h):
+            dst = grouped[:].rearrange("p (t m j) -> p m t j", t=PACK, j=PACK)[:, h * 64 : (h + 1) * 64]
+            copy(dst, raw[:].rearrange("p j (m t) -> p m t j", t=PACK))
+
+        def scalar_copy(dst, src):
+            nc.scalar.activation(dst, src, COPY)
+
+        def quantize_by_tile(grouped, name):
+            codes = sb([P, N], U32, name + "_codes")
+            scales = sb([P, N], U8, name + "_scales")
+            for t in range(PACK):
+                cols = slice(t * P, (t + 1) * P)
+                nc.vector.quantize_mx(codes[:, cols].bitcast(FP8X4), scales[:, cols], grouped[:, t * 512 : (t + 1) * 512])
+            return codes, scales
+
+        def product(acc, w_codes, w_scales, t, codes, scales):
+            cols = slice(t * P, (t + 1) * P)
+            nc.tensor.matmul_mx(acc, lhsT=w_codes[:, cols].bitcast(FP8X4), lhsT_scale=w_scales[:, cols],
+                                rhs=codes.bitcast(FP8X4), rhs_scale=scales, start=True, stop=True)
+
+        mds_t = load_list(mds, "mds_t")
+        e_word_table = load_word_table(e_words, "e_word_table")
+        e_scale_table = scale_table("e_scale_table")
+        x_scale_table = scale_table("x_scale_table")
+        load_scale_rows(nc.sync, e_scale_table, e_scales, range(4))
+        load_scale_rows(nc.gpsimd, x_scale_table, x_scales, (0, 1))
+        w2_raw = [load_weight_half(w2, h, "w2_raw%d" % h) for h in range(2)]
+        x_word_table = load_word_table(x_words, "x_word_table")
+        offs_t = load_list(offs, "offs_t")
+        md_t = load_list(md, "md_t")
+        load_scale_rows(nc.sync, x_scale_table, x_scales, (2, 3))
+        w1_raw = [load_weight_half(w1, h, "w1_raw%d" % h) for h in range(2)]
+        prv_t = load_list(prv, "prv_t")
+        unit_t = sb([P, PACK], F32, "unit_t")
+        nc.sync.dma_start(unit_t[:], unit.rearrange("(p t) o -> p (t o)", t=PACK))
+        w3_raw = [load_weight_half(w3, h, "w3_raw%d" % h) for h in range(2)]
+        minus_unit = sb([P, PACK], F32, "minus_unit")
+        nc.gpsimd.tensor_scalar(minus_unit[:], unit_t[:], -1.0, 0.0, ALU.mult, ALU.add)
+
+        e_codes = sb([P, S], U32, "e_codes")
+        e_bytes = sb([P, S], U8, "e_bytes")
+        nc.vector.tensor_copy(e_bytes[:], e_scale_table[:].indirect(mds_t[:]))
+        nc.vector.tensor_copy(e_codes[:], e_word_table[:].bitcast(U32).indirect(mds_t[:]))
+        w2_grouped = sb([P, PACK * N], BF16, "w2_grouped")
+        deal(scalar_copy, w2_grouped, w2_raw[0], 0)
+        deal(nc.vector.tensor_copy, w2_grouped, w2_raw[1], 1)
+        w2_codes, w2_scales = quantize_by_tile(w2_grouped, "w2")
+        ye_acc = [psum.tile([P, S], F32, name="ye_acc%d" % t, tag="bank%d" % t) for t in range(PACK)]
+        for t in range(PACK):
+            product(ye_acc[t][:], w2_codes, w2_scales, t, e_codes[:], e_bytes[:])
+
+        x_codes = sb([P, S], U32, "x_codes")
+        x_bytes = sb([P, S], U8, "x_bytes")
+        nc.vector.tensor_copy(x_codes[:], x_word_table[:].bitcast(U32).indirect(offs_t[:]))
+        nc.vector.tensor_copy(x_bytes[:], x_scale_table[:].indirect(offs_t[:]))
+        w1_grouped = sb([P, PACK * N], BF16, "w1_grouped")
+        for h in range(2):
+            deal(nc.vector.tensor_copy, w1_grouped, w1_raw[h], h)
+        w1_codes, w1_scales = quantize_by_tile(w1_grouped, "w1")
+        y_acc = [psum.tile([P, S], F32, name="y_acc%d" % t) for t in range(PACK)]
+        for t in range(PACK):
+            product(y_acc[t][:], w1_codes, w1_scales, t, x_codes[:], x_bytes[:])
+
+        em = sb([P, PACK, S], F32, "em")
+        res1 = [sb([P, S], F32, "res1_%d" % t) for t in range(PACK)]
+        gap = [sb([P, PACK, hi - lo], F32, "gap%d" % c) for c, (lo, hi) in enumerate(CHUNKS)]
+        hid = [sb([P, PACK, hi - lo], F32, "hid%d" % c) for c, (lo, hi) in enumerate(CHUNKS)]
+        hid_grouped = [sb([P, hi - lo, PACK], BF16, "hid_grouped%d" % c) for c, (lo, hi) in enumerate(CHUNKS)]
+        h_codes = sb([P, S], U32, "h_codes")
+        h_scales = sb([P, S], U8, "h_scales")
+        result = [sb([P, PACK, hi - lo], F32, "result%d" % c) for c, (lo, hi) in enumerate(CHUNKS)]
+        w3_grouped = sb([P, PACK * N], BF16, "w3_grouped")
+        w3_codes = sb([P, N], U32, "w3_codes")
+        w3_scales = sb([P, N], U8, "w3_scales")
+        o_codes = sb([P, S], U32, "o_codes")
+        o_scales = sb([P, S], U8, "o_scales")
+        out_rows = out_0.rearrange("(p t) n -> p t n", t=PACK)
+        out_words = out_1[0].rearrange("p n t -> p (n t)").bitcast(I32)
+
+        def make_em(t):
+            ye = sb([P, S], F32, "ye%d" % t)
+            nc.scalar.copy(ye[:], ye_acc[t][:])
+            for h in range(2):
+                nc.scalar.activation(em[:, t, h * HALF : (h + 1) * HALF], ye[:].indirect(md_t[:, h * 16 : (h + 1) * 16]), COPY)
+
+        def make_res1(t):
+            nc.vector.tensor_tensor(res1[t][:], y_acc[t][:], em[:, t, :], ALU.add)
+
+        def looked_up(t, c):
+            lo, hi = CHUNKS[c]
+            return res1[t][:].indirect(prv_t[:, lo // 16 : hi // 16])
+
+        def fused_gap(t, c):
+            nc.vector.tensor_tensor(gap[c][:, t, :], looked_up(t, c), em[:, t, slice(*CHUNKS[c])], ALU.subtract)
+
+        def fetch_rp(c):
+            for t in range(PACK):
+                nc.scalar.activation(gap[c][:, t, :], looked_up(t, c), COPY)
+
+        def plain_gap(c):
+            nc.vector.tensor_tensor(gap[c][:], gap[c][:], em[:, :, slice(*CHUNKS[c])], ALU.subtract)
+
+        def clip_gap(t, c):
+            nc.vector.tensor_scalar(gap[c][:, t, :], gap[c][:, t, :], 0.0, unit_t[:, t : t + 1], ALU.max, ALU.mult)
+
+        def make_hid(t, c):
+            nc.vector.scalar_tensor_tensor(hid[c][:, t, :], y_acc[t][:, slice(*CHUNKS[c])], minus_unit[:, t : t + 1], gap[c][:, t, :], ALU.mult, ALU.add)
+
+        def group_hid(c, copy):
+            copy(hid_grouped[c][:], hid[c][:].rearrange("p t n -> p n t"))
+
+        def last_product(c):
+            lo, hi = CHUNKS[c]
+            n = hi - lo
+            cols = slice(lo, hi)
+            nc.vector.quantize_mx(h_codes[:, cols].bitcast(FP8X4), h_scales[:, cols], hid_grouped[c][:].rearrange("p n t -> p (n t)"))
+            per_bank = 512 // n
+            for b in range(PACK // per_bank):
+                acc = psum.tile([P, per_bank, n], F32, name="out_acc%d_%d" % (c, b), tag="bank%d" % (lo // P + b))
+                for u in range(per_bank):
+                    product(acc[:, u, :], w3_codes, w3_scales, per_bank * b + u, h_codes[:, cols], h_scales[:, cols])
+                nc.scalar.copy(result[c][:, per_bank * b : per_bank * (b + 1), :], acc[:])
+            nc.sync.dma_start(out_rows[:, :, cols], result[c][:])
+
+        def make_planes(c):
+            lo, hi = CHUNKS[c]
+            cols = slice(lo, hi)
+            out_grouped = sb([P, hi - lo, PACK], BF16, "out_grouped%d" % c)
+            nc.vector.tensor_copy(out_grouped[:], result[c][:].rearrange("p t n -> p n t"))
+            nc.vector.quantize_mx(o_codes[:, cols].bitcast(FP8X4), o_scales[:, cols], out_grouped[:].rearrange("p n t -> p (n t)"))
+            nc.sync.dma_start(out_words[:, cols], o_codes[:, cols].bitcast(I32))
+
+        for t in range(PACK):
+            make_em(t)
+        make_res1(0)
+        make_res1(1)
+        fused_gap(0, 0)
+        fused_gap(1, 0)
+        make_res1(2)
+        for step in (clip_gap, make_hid):
+            for t in (0, 1):
+                step(t, 0)
+        fused_gap(2, 0)
+        make_res1(3)
+        clip_gap(2, 0)
+        fused_gap(3, 0)
+        make_hid(2, 0)
+        clip_gap(3, 0)
+        for h in range(2):
+            deal(scalar_copy, w3_grouped, w3_raw[h], h)
+        nc.vector.quantize_mx(w3_codes[:].bitcast(FP8X4), w3_scales[:], w3_grouped[:])
+        make_hid(3, 0)
+        fetch_rp(1)
+        group_hid(0, nc.scalar.copy)
+        fetch_rp(2)
+        plain_gap(1)
+        for step in (clip_gap, make_hid):
+            for t in range(PACK):
+                step(t, 1)
+        last_product(0)
+        group_hid(1, nc.scalar.copy)
+        plain_gap(2)
+        for step in (clip_gap, make_hid):
+            for t in range(PACK):
+                step(t, 2)
+        last_product(1)
+        group_hid(2, nc.vector.tensor_copy)
+        make_planes(0)
+        last_product(2)
+        make_planes(1)
+        make_planes(2)
+        for q in range(4):
+            queue = nc.sync if q % 2 else nc.scalar
+            queue.dma_start(out_2[0, 4 * q : 4 * q + 4, :].bitcast(I32), o_scales[32 * q : 32 * q + 4, :].bitcast(I32))

@@ -52,60 +52,69 @@ def tile_picked_ytransc_max_po_kernel(
             nc.sync.dma_start(tile[:], src[0].rearrange("p n t -> p (n t)").bitcast(I32))
             return tile
 
-        def load_weight_half(w, h, name):
-            tile = sb([P, PACK, HALF], F32, name)
-            nc.sync.dma_start(tile[:], w.rearrange("(p j) c -> p j c", j=PACK)[:, :, h * HALF : (h + 1) * HALF])
+        def load_weight(w, name):
+            tile = sb([P, PACK, N], F32, name)
+            nc.sync.dma_start(tile[:], w.rearrange("(p j) c -> p j c", j=PACK))
             return tile
 
-        def deal(copy, grouped, raw, h):
-            dst = grouped[:].rearrange("p (t m j) -> p m t j", t=PACK, j=PACK)[:, h * 64 : (h + 1) * 64]
-            copy(dst, raw[:].rearrange("p j (m t) -> p m t j", t=PACK))
+        def deal(copy, grouped, raw, lo, hi):
+            dst = grouped[:].rearrange("p (t m j) -> p m t j", t=PACK, j=PACK)[:, lo:hi]
+            copy(dst, raw[:].rearrange("p j (m t) -> p m t j", t=PACK)[:, lo:hi])
+
+        def load_hidden_rows(queue, src, width, name):
+            tile = sb([P, PACK, width], F32, name)
+            rows = src.rearrange("(c t r) n -> r c t n", t=PACK, r=4)
+            for r in range(4):
+                queue.dma_start(tile[r:P:4], rows[r])
+            return tile
+
+        def round_tile(copy, grouped, raw, t):
+            dst = grouped[:].rearrange("p (t c r j) -> p t c j r", t=PACK, r=4, j=PACK)[:, t]
+            copy(dst, raw[:].rearrange("p j (c t r) -> p t c j r", t=PACK, r=4)[:, t])
+
+        def quantize_tile(codes, scales, grouped, t):
+            cols = slice(t * P, (t + 1) * P)
+            nc.vector.quantize_mx(codes[:, cols].bitcast(FP8X4), scales[:, cols], grouped[:, t * 512 : (t + 1) * 512])
 
         def scalar_copy(dst, src):
             nc.scalar.activation(dst, src, COPY)
-
-        def quantize_by_tile(grouped, name):
-            codes = sb([P, N], U32, name + "_codes")
-            scales = sb([P, N], U8, name + "_scales")
-            for t in range(PACK):
-                cols = slice(t * P, (t + 1) * P)
-                nc.vector.quantize_mx(codes[:, cols].bitcast(FP8X4), scales[:, cols], grouped[:, t * 512 : (t + 1) * 512])
-            return codes, scales
 
         def product(acc, w_codes, w_scales, t, codes, scales):
             cols = slice(t * P, (t + 1) * P)
             nc.tensor.matmul_mx(acc, lhsT=w_codes[:, cols].bitcast(FP8X4), lhsT_scale=w_scales[:, cols],
                                 rhs=codes.bitcast(FP8X4), rhs_scale=scales, start=True, stop=True)
 
+        on_v, on_s = nc.vector.tensor_copy, nc.scalar.copy
+        W2ENG = (on_v, on_s, on_v, on_s)
+        W1ENG = (on_v, on_v, on_v, on_v)
         mds_t = load_list(mds, "mds_t")
         e_word_table = load_word_table(e_words, "e_word_table")
+        offs_t = load_list(offs, "offs_t")
         e_scale_table = scale_table("e_scale_table")
         x_scale_table = scale_table("x_scale_table")
         load_scale_rows(nc.sync, e_scale_table, e_scales, range(4))
-        load_scale_rows(nc.gpsimd, x_scale_table, x_scales, (0, 1))
-        w2_raw = [load_weight_half(w2, h, "w2_raw%d" % h) for h in range(2)]
+        w2_raw = load_weight(w2, "w2_raw")
         x_word_table = load_word_table(x_words, "x_word_table")
-        offs_t = load_list(offs, "offs_t")
         md_t = load_list(md, "md_t")
-        load_scale_rows(nc.sync, x_scale_table, x_scales, (2, 3))
-        w1_raw = [load_weight_half(w1, h, "w1_raw%d" % h) for h in range(2)]
+        load_scale_rows(nc.sync, x_scale_table, x_scales, range(4))
+        w1_raw = load_weight(w1, "w1_raw")
         prv_t = load_list(prv, "prv_t")
-        unit_t = sb([P, PACK], F32, "unit_t")
-        nc.sync.dma_start(unit_t[:], unit.rearrange("(p t) o -> p (t o)", t=PACK))
-        w3_raw = [load_weight_half(w3, h, "w3_raw%d" % h) for h in range(2)]
-        minus_unit = sb([P, PACK], F32, "minus_unit")
-        nc.gpsimd.tensor_scalar(minus_unit[:], unit_t[:], -1.0, 0.0, ALU.mult, ALU.add)
+        w3_raw = load_hidden_rows(nc.sync, w3, N, "w3_raw")
+        with nc.allow_non_contiguous_dma(reason="one factor for each hidden row"):
+            unit_t = load_hidden_rows(nc.sync, unit, 1, "unit_t")
 
         e_codes = sb([P, S], U32, "e_codes")
         e_bytes = sb([P, S], U8, "e_bytes")
         nc.vector.tensor_copy(e_bytes[:], e_scale_table[:].indirect(mds_t[:]))
         nc.vector.tensor_copy(e_codes[:], e_word_table[:].bitcast(U32).indirect(mds_t[:]))
         w2_grouped = sb([P, PACK * N], BF16, "w2_grouped")
-        deal(scalar_copy, w2_grouped, w2_raw[0], 0)
-        deal(nc.vector.tensor_copy, w2_grouped, w2_raw[1], 1)
-        w2_codes, w2_scales = quantize_by_tile(w2_grouped, "w2")
+        w2_codes = sb([P, N], U32, "w2_codes")
+        w2_scales = sb([P, N], U8, "w2_scales")
         ye_acc = [psum.tile([P, S], F32, name="ye_acc%d" % t, tag="bank%d" % t) for t in range(PACK)]
         for t in range(PACK):
+            round_tile(W2ENG[t], w2_grouped, w2_raw, t)
+        for t in range(PACK):
+            quantize_tile(w2_codes, w2_scales, w2_grouped, t)
             product(ye_acc[t][:], w2_codes, w2_scales, t, e_codes[:], e_bytes[:])
 
         x_codes = sb([P, S], U32, "x_codes")
@@ -113,12 +122,15 @@ def tile_picked_ytransc_max_po_kernel(
         nc.vector.tensor_copy(x_codes[:], x_word_table[:].bitcast(U32).indirect(offs_t[:]))
         nc.vector.tensor_copy(x_bytes[:], x_scale_table[:].indirect(offs_t[:]))
         w1_grouped = sb([P, PACK * N], BF16, "w1_grouped")
-        for h in range(2):
-            deal(nc.vector.tensor_copy, w1_grouped, w1_raw[h], h)
-        w1_codes, w1_scales = quantize_by_tile(w1_grouped, "w1")
+        w1_codes = sb([P, N], U32, "w1_codes")
+        w1_scales = sb([P, N], U8, "w1_scales")
         y_acc = [psum.tile([P, S], F32, name="y_acc%d" % t) for t in range(PACK)]
-        for t in range(PACK):
-            product(y_acc[t][:], w1_codes, w1_scales, t, x_codes[:], x_bytes[:])
+        for t in range(PACK + 1):
+            if t < PACK:
+                round_tile(W1ENG[t], w1_grouped, w1_raw, t)
+            if t:
+                quantize_tile(w1_codes, w1_scales, w1_grouped, t - 1)
+                product(y_acc[t - 1][:], w1_codes, w1_scales, t - 1, x_codes[:], x_bytes[:])
 
         em = sb([P, PACK, S], F32, "em")
         res1 = [sb([P, S], F32, "res1_%d" % t) for t in range(PACK)]
@@ -152,81 +164,95 @@ def tile_picked_ytransc_max_po_kernel(
         def fused_gap(t, c):
             nc.vector.tensor_tensor(gap[c][:, t, :], looked_up(t, c), em[:, t, slice(*CHUNKS[c])], ALU.subtract)
 
-        def fetch_rp(c):
-            for t in range(PACK):
-                nc.scalar.activation(gap[c][:, t, :], looked_up(t, c), COPY)
+        def fetch_rp(t, c):
+            nc.scalar.activation(gap[c][:, t, :], looked_up(t, c), COPY)
 
-        def plain_gap(c):
-            nc.vector.tensor_tensor(gap[c][:], gap[c][:], em[:, :, slice(*CHUNKS[c])], ALU.subtract)
-
-        def clip_gap(t, c):
-            nc.vector.tensor_scalar(gap[c][:, t, :], gap[c][:, t, :], 0.0, unit_t[:, t : t + 1], ALU.max, ALU.mult)
+        def plain_gap(c, ts):
+            nc.vector.tensor_tensor(gap[c][:, ts, :], gap[c][:, ts, :], em[:, ts, slice(*CHUNKS[c])], ALU.subtract)
 
         def make_hid(t, c):
-            nc.vector.scalar_tensor_tensor(hid[c][:, t, :], y_acc[t][:, slice(*CHUNKS[c])], minus_unit[:, t : t + 1], gap[c][:, t, :], ALU.mult, ALU.add)
+            nc.vector.scalar_tensor_tensor(hid[c][:, t, :], gap[c][:, t, :], 0.0, y_acc[t][:, slice(*CHUNKS[c])], ALU.max, ALU.subtract)
 
-        def group_hid(c, copy):
-            copy(hid_grouped[c][:], hid[c][:].rearrange("p t n -> p n t"))
+        minus_unit = unit_t
+
+        def clip_gap(t, c):
+            nc.vector.tensor_scalar(gap[c][:, t, :], gap[c][:, t, :], 0.0, unit_t[:, t, :], ALU.max, ALU.mult)
+
+        def scaled_hid(t, c):
+            nc.vector.scalar_tensor_tensor(hid[c][:, t, :], y_acc[t][:, slice(*CHUNKS[c])], minus_unit[:, t, :], gap[c][:, t, :], ALU.mult, ALU.add)
+
+        def by_line(grouped, plain):
+            return (grouped[:].rearrange("p (c i) t -> p c t i", i=4), plain[:].rearrange("p t (c i) -> p c t i", i=4))
+
+        def group_hid(c):
+            dst, src = by_line(hid_grouped[c], hid[c])
+            factor = unit_t[:].unsqueeze(1).to_broadcast(list(src.shape))
+            nc.vector.tensor_tensor(dst, src, factor, ALU.mult)
 
         def last_product(c):
             lo, hi = CHUNKS[c]
             n = hi - lo
             cols = slice(lo, hi)
             nc.vector.quantize_mx(h_codes[:, cols].bitcast(FP8X4), h_scales[:, cols], hid_grouped[c][:].rearrange("p n t -> p (n t)"))
-            per_bank = 512 // n
+            per_bank = 2
             for b in range(PACK // per_bank):
-                acc = psum.tile([P, per_bank, n], F32, name="out_acc%d_%d" % (c, b), tag="bank%d" % (lo // P + b))
+                acc = psum.tile([P, per_bank, n], F32, name="out_acc%d_%d" % (c, b), tag="bank%d" % ((2 * c + b) % 4))
                 for u in range(per_bank):
                     product(acc[:, u, :], w3_codes, w3_scales, per_bank * b + u, h_codes[:, cols], h_scales[:, cols])
-                nc.scalar.copy(result[c][:, per_bank * b : per_bank * (b + 1), :], acc[:])
+                (on_v if c == 2 and b == 1 else on_s)(result[c][:, per_bank * b : per_bank * (b + 1), :], acc[:])
             nc.sync.dma_start(out_rows[:, :, cols], result[c][:])
 
+        out_grouped = [sb([P, hi - lo, PACK], BF16, "out_grouped%d" % c) for c, (lo, hi) in enumerate(CHUNKS)]
+
+        def group_planes(c, copy):
+            copy(*by_line(out_grouped[c], result[c]))
+
         def make_planes(c):
-            lo, hi = CHUNKS[c]
-            cols = slice(lo, hi)
-            out_grouped = sb([P, hi - lo, PACK], BF16, "out_grouped%d" % c)
-            nc.vector.tensor_copy(out_grouped[:], result[c][:].rearrange("p t n -> p n t"))
-            nc.vector.quantize_mx(o_codes[:, cols].bitcast(FP8X4), o_scales[:, cols], out_grouped[:].rearrange("p n t -> p (n t)"))
+            cols = slice(*CHUNKS[c])
+            nc.vector.quantize_mx(o_codes[:, cols].bitcast(FP8X4), o_scales[:, cols], out_grouped[c][:].rearrange("p n t -> p (n t)"))
             nc.sync.dma_start(out_words[:, cols], o_codes[:, cols].bitcast(I32))
 
         for t in range(PACK):
             make_em(t)
+        deal(scalar_copy, w3_grouped, w3_raw, 0, P)
         make_res1(0)
         make_res1(1)
         fused_gap(0, 0)
         fused_gap(1, 0)
         make_res1(2)
-        for step in (clip_gap, make_hid):
-            for t in (0, 1):
-                step(t, 0)
-        fused_gap(2, 0)
+        make_hid(0, 0)
+        make_hid(1, 0)
         make_res1(3)
-        clip_gap(2, 0)
+        fused_gap(2, 0)
         fused_gap(3, 0)
+        for t in range(PACK):
+            fetch_rp(t, 1)
         make_hid(2, 0)
-        clip_gap(3, 0)
-        for h in range(2):
-            deal(scalar_copy, w3_grouped, w3_raw[h], h)
-        nc.vector.quantize_mx(w3_codes[:].bitcast(FP8X4), w3_scales[:], w3_grouped[:])
         make_hid(3, 0)
-        fetch_rp(1)
-        group_hid(0, nc.scalar.copy)
-        fetch_rp(2)
-        plain_gap(1)
-        for step in (clip_gap, make_hid):
-            for t in range(PACK):
-                step(t, 1)
+        for t in range(PACK):
+            fetch_rp(t, 2)
+        nc.vector.quantize_mx(w3_codes[:].bitcast(FP8X4), w3_scales[:], w3_grouped[:])
+        group_hid(0)
+        plain_gap(1, slice(0, 4))
         last_product(0)
-        group_hid(1, nc.scalar.copy)
-        plain_gap(2)
-        for step in (clip_gap, make_hid):
-            for t in range(PACK):
-                step(t, 2)
+        make_hid(0, 1)
+        make_hid(1, 1)
+        make_hid(2, 1)
+        make_hid(3, 1)
+        group_planes(0, on_s)
+        plain_gap(2, slice(0, 4))
+        group_hid(1)
+        make_hid(0, 2)
+        make_hid(1, 2)
         last_product(1)
-        group_hid(2, nc.vector.tensor_copy)
+        group_planes(1, on_s)
+        make_hid(2, 2)
+        make_hid(3, 2)
         make_planes(0)
+        group_hid(2)
         last_product(2)
         make_planes(1)
+        group_planes(2, on_v)
         make_planes(2)
         for q in range(4):
             queue = nc.sync if q % 2 else nc.scalar

@@ -2,7 +2,7 @@ from contextlib import ExitStack
 
 import concourse.mybir as mybir
 
-K, T, S, N = 512, 1024, 512, 512
+T, S, N = 1024, 512, 512
 FLOPS = 3 * 2 * 512 * 512 * 512
 
 F32 = mybir.dt.float32
@@ -18,7 +18,7 @@ COPY = mybir.ActivationFunctionType.Copy
 P = 128
 PACK = 4
 HALF = 256
-CHUNKS = ((0, 256), (256, 384), (384, 512))
+CHUNK = 128
 
 
 def tile_picked_ytransc_max_po_kernel(
@@ -29,23 +29,25 @@ def tile_picked_ytransc_max_po_kernel(
         lists = ctx.enter_context(tc.tile_pool(name="lists", bufs=1))
         keep = ctx.enter_context(tc.tile_pool(name="keep", bufs=1))
         psum = ctx.enter_context(tc.psum_pool(name="psum", bufs=1))
+        on_v, on_s = nc.vector.tensor_copy, nc.scalar.copy
 
-        def sb(shape, dtype, name):
-            return keep.tile(shape, dtype, name=name, align_bytes=64)
+        def on_g(dst, src):
+            nc.gpsimd.tensor_scalar(dst, src, 1.0, 0.0, ALU.mult, ALU.add)
+
+        def sb(shape, dtype, name, tag=""):
+            return keep.tile(shape, dtype, name=name, tag=tag or name, align_bytes=64)
 
         def load_list(src, name):
             tile = lists.tile([P, S // 16], U16, name=name)
             nc.sync.dma_start(tile[:], src)
             return tile
 
-        def scale_table(name):
+        def load_scale_table(src, name):
             tile = sb([P, T], U8, name)
             nc.gpsimd.memset(tile[:].bitcast(I32), 0)
+            for q in range(4):
+                nc.sync.dma_start(tile[32 * q : 32 * q + 4, :].bitcast(I32), src[0, 4 * q : 4 * q + 4, :].bitcast(I32))
             return tile
-
-        def load_scale_rows(queue, tile, src, quadrants):
-            for q in quadrants:
-                queue.dma_start(tile[32 * q : 32 * q + 4, :].bitcast(I32), src[0, 4 * q : 4 * q + 4, :].bitcast(I32))
 
         def load_word_table(src, name):
             tile = sb([P, T], I32, name)
@@ -57,89 +59,81 @@ def tile_picked_ytransc_max_po_kernel(
             nc.sync.dma_start(tile[:], w.rearrange("(p j) c -> p j c", j=PACK))
             return tile
 
-        def deal(copy, grouped, raw, lo, hi):
-            dst = grouped[:].rearrange("p (t m j) -> p m t j", t=PACK, j=PACK)[:, lo:hi]
-            copy(dst, raw[:].rearrange("p j (m t) -> p m t j", t=PACK)[:, lo:hi])
-
-        def load_hidden_rows(queue, src, width, name):
+        def load_hidden_rows(src, width, name):
             tile = sb([P, PACK, width], F32, name)
             rows = src.rearrange("(c t r) n -> r c t n", t=PACK, r=4)
             for r in range(4):
-                queue.dma_start(tile[r:P:4], rows[r])
+                nc.sync.dma_start(tile[r:P:4], rows[r])
             return tile
 
-        def round_tile(copy, grouped, raw, t):
-            dst = grouped[:].rearrange("p (t c r j) -> p t c j r", t=PACK, r=4, j=PACK)[:, t]
-            copy(dst, raw[:].rearrange("p j (c t r) -> p t c j r", t=PACK, r=4)[:, t])
+        def round_tile(copy, grouped, raw, t, order="p t c j r"):
+            dst = grouped[:].rearrange("p (t c r j) -> " + order, t=PACK, r=4, j=PACK)[:, t]
+            copy(dst, raw[:].rearrange("p j (c t r) -> " + order, t=PACK, r=4)[:, t])
+
+        def quantize(codes, scales, grouped):
+            nc.vector.quantize_mx(codes.bitcast(FP8X4), scales, grouped)
 
         def quantize_tile(codes, scales, grouped, t):
             cols = slice(t * P, (t + 1) * P)
-            nc.vector.quantize_mx(codes[:, cols].bitcast(FP8X4), scales[:, cols], grouped[:, t * 512 : (t + 1) * 512])
-
-        def scalar_copy(dst, src):
-            nc.scalar.activation(dst, src, COPY)
+            quantize(codes[:, cols], scales[:, cols], grouped[:, t * 512 : (t + 1) * 512])
 
         def product(acc, w_codes, w_scales, t, codes, scales):
             cols = slice(t * P, (t + 1) * P)
             nc.tensor.matmul_mx(acc, lhsT=w_codes[:, cols].bitcast(FP8X4), lhsT_scale=w_scales[:, cols],
                                 rhs=codes.bitcast(FP8X4), rhs_scale=scales, start=True, stop=True)
 
-        on_v, on_s = nc.vector.tensor_copy, nc.scalar.copy
-        W2ENG = (on_v, on_s, on_v, on_s)
-        W1ENG = (on_v, on_v, on_v, on_v)
         mds_t = load_list(mds, "mds_t")
         e_word_table = load_word_table(e_words, "e_word_table")
         offs_t = load_list(offs, "offs_t")
-        e_scale_table = scale_table("e_scale_table")
-        x_scale_table = scale_table("x_scale_table")
-        load_scale_rows(nc.sync, e_scale_table, e_scales, range(4))
+        e_scale_table = load_scale_table(e_scales, "e_scale_table")
         w2_raw = load_weight(w2, "w2_raw")
         x_word_table = load_word_table(x_words, "x_word_table")
         md_t = load_list(md, "md_t")
-        load_scale_rows(nc.sync, x_scale_table, x_scales, range(4))
+        x_scale_table = load_scale_table(x_scales, "x_scale_table")
         w1_raw = load_weight(w1, "w1_raw")
         prv_t = load_list(prv, "prv_t")
-        w3_raw = load_hidden_rows(nc.sync, w3, N, "w3_raw")
         with nc.allow_non_contiguous_dma(reason="one factor for each hidden row"):
-            unit_t = load_hidden_rows(nc.sync, unit, 1, "unit_t")
+            unit_t = load_hidden_rows(unit, 1, "unit_t")
+        w3_raw = load_hidden_rows(w3, N, "w3_raw")
 
         e_codes = sb([P, S], U32, "e_codes")
         e_bytes = sb([P, S], U8, "e_bytes")
-        nc.vector.tensor_copy(e_bytes[:], e_scale_table[:].indirect(mds_t[:]))
         nc.vector.tensor_copy(e_codes[:], e_word_table[:].bitcast(U32).indirect(mds_t[:]))
+        nc.vector.tensor_copy(e_bytes[:], e_scale_table[:].indirect(mds_t[:]))
         w2_grouped = sb([P, PACK * N], BF16, "w2_grouped")
         w2_codes = sb([P, N], U32, "w2_codes")
         w2_scales = sb([P, N], U8, "w2_scales")
         ye_acc = [psum.tile([P, S], F32, name="ye_acc%d" % t, tag="bank%d" % t) for t in range(PACK)]
         for t in range(PACK):
-            round_tile(W2ENG[t], w2_grouped, w2_raw, t)
+            round_tile(on_s if t % 2 else on_v, w2_grouped, w2_raw, t)
         for t in range(PACK):
             quantize_tile(w2_codes, w2_scales, w2_grouped, t)
             product(ye_acc[t][:], w2_codes, w2_scales, t, e_codes[:], e_bytes[:])
 
         x_codes = sb([P, S], U32, "x_codes")
         x_bytes = sb([P, S], U8, "x_bytes")
-        nc.vector.tensor_copy(x_codes[:], x_word_table[:].bitcast(U32).indirect(offs_t[:]))
-        nc.vector.tensor_copy(x_bytes[:], x_scale_table[:].indirect(offs_t[:]))
         w1_grouped = sb([P, PACK * N], BF16, "w1_grouped")
         w1_codes = sb([P, N], U32, "w1_codes")
         w1_scales = sb([P, N], U8, "w1_scales")
         y_acc = [psum.tile([P, S], F32, name="y_acc%d" % t) for t in range(PACK)]
+        nc.vector.tensor_copy(x_codes[:], x_word_table[:].bitcast(U32).indirect(offs_t[:]))
+        nc.vector.tensor_copy(x_bytes[:], x_scale_table[:].indirect(offs_t[:]))
         for t in range(PACK + 1):
             if t < PACK:
-                round_tile(W1ENG[t], w1_grouped, w1_raw, t)
+                round_tile(on_v, w1_grouped, w1_raw, t)
             if t:
                 quantize_tile(w1_codes, w1_scales, w1_grouped, t - 1)
                 product(y_acc[t - 1][:], w1_codes, w1_scales, t - 1, x_codes[:], x_bytes[:])
 
         em = sb([P, PACK, S], F32, "em")
         res1 = [sb([P, S], F32, "res1_%d" % t) for t in range(PACK)]
-        gap = [sb([P, PACK, hi - lo], F32, "gap%d" % c) for c, (lo, hi) in enumerate(CHUNKS)]
-        hid = [sb([P, PACK, hi - lo], F32, "hid%d" % c) for c, (lo, hi) in enumerate(CHUNKS)]
-        hid_grouped = [sb([P, hi - lo, PACK], BF16, "hid_grouped%d" % c) for c, (lo, hi) in enumerate(CHUNKS)]
+        gap = [sb([P, PACK, HALF], F32, "gap0")]
+        hid = [sb([P, PACK, HALF], F32, "hid%d" % h) for h in range(2)]
+        hid_grouped = [sb([P, CHUNK, PACK], BF16, "hid_grouped%d" % c) for c in range(4)]
         h_codes = sb([P, S], U32, "h_codes")
         h_scales = sb([P, S], U8, "h_scales")
-        result = [sb([P, PACK, hi - lo], F32, "result%d" % c) for c, (lo, hi) in enumerate(CHUNKS)]
+        result = [sb([P, PACK, CHUNK], F32, "result%d" % c) for c in range(4)]
+        out_grouped = [sb([P, CHUNK, PACK], BF16, "out_grouped%d" % c) for c in range(4)]
         w3_grouped = sb([P, PACK * N], BF16, "w3_grouped")
         w3_codes = sb([P, N], U32, "w3_codes")
         w3_scales = sb([P, N], U8, "w3_scales")
@@ -148,112 +142,129 @@ def tile_picked_ytransc_max_po_kernel(
         out_rows = out_0.rearrange("(p t) n -> p t n", t=PACK)
         out_words = out_1[0].rearrange("p n t -> p (n t)").bitcast(I32)
 
+        def part(tiles, ts, lo, hi):
+            if tiles is gap and lo >= 384:
+                return last_gap[:, ts, :]
+            return tiles[lo // HALF][:, ts, lo % HALF : lo % HALF + hi - lo]
+
         def make_em(t):
             ye = sb([P, S], F32, "ye%d" % t)
             nc.scalar.copy(ye[:], ye_acc[t][:])
             for h in range(2):
                 nc.scalar.activation(em[:, t, h * HALF : (h + 1) * HALF], ye[:].indirect(md_t[:, h * 16 : (h + 1) * 16]), COPY)
 
+        def round_w3(copy, lo, hi):
+            dst = w3_grouped[:].rearrange("p (t m j) -> p m t j", t=PACK, j=PACK)[:, lo:hi]
+            copy(dst, w3_raw[:].rearrange("p j (m t) -> p m t j", t=PACK)[:, lo:hi])
+
         def make_res1(t):
             nc.vector.tensor_tensor(res1[t][:], y_acc[t][:], em[:, t, :], ALU.add)
 
-        def looked_up(t, c):
-            lo, hi = CHUNKS[c]
+        def looked_up(t, lo, hi):
             return res1[t][:].indirect(prv_t[:, lo // 16 : hi // 16])
 
-        def fused_gap(t, c):
-            nc.vector.tensor_tensor(gap[c][:, t, :], looked_up(t, c), em[:, t, slice(*CHUNKS[c])], ALU.subtract)
+        def fused_gap(t, lo, hi):
+            nc.vector.tensor_tensor(part(gap, t, lo, hi), looked_up(t, lo, hi), em[:, t, lo:hi], ALU.subtract)
 
-        def fetch_rp(t, c):
-            nc.scalar.activation(gap[c][:, t, :], looked_up(t, c), COPY)
+        def fetch_rp(t, lo, hi):
+            nc.scalar.activation(part(gap, t, lo, hi), looked_up(t, lo, hi), COPY)
 
-        def plain_gap(c, ts):
-            nc.vector.tensor_tensor(gap[c][:, ts, :], gap[c][:, ts, :], em[:, ts, slice(*CHUNKS[c])], ALU.subtract)
+        def fetch_rp_v(t, lo, hi):
+            nc.vector.tensor_copy(part(gap, t, lo, hi), looked_up(t, lo, hi))
 
-        def make_hid(t, c):
-            nc.vector.scalar_tensor_tensor(hid[c][:, t, :], gap[c][:, t, :], 0.0, y_acc[t][:, slice(*CHUNKS[c])], ALU.max, ALU.subtract)
+        def plain_gap(ts, lo, hi):
+            nc.vector.tensor_tensor(part(gap, ts, lo, hi), part(gap, ts, lo, hi), em[:, ts, lo:hi], ALU.subtract)
 
-        minus_unit = unit_t
-
-        def clip_gap(t, c):
-            nc.vector.tensor_scalar(gap[c][:, t, :], gap[c][:, t, :], 0.0, unit_t[:, t, :], ALU.max, ALU.mult)
-
-        def scaled_hid(t, c):
-            nc.vector.scalar_tensor_tensor(hid[c][:, t, :], y_acc[t][:, slice(*CHUNKS[c])], minus_unit[:, t, :], gap[c][:, t, :], ALU.mult, ALU.add)
+        def make_hid(t, lo, hi):
+            nc.vector.scalar_tensor_tensor(part(hid, t, lo, hi), part(gap, t, lo, hi), 0.0, y_acc[t][:, lo:hi], ALU.max, ALU.subtract)
 
         def by_line(grouped, plain):
-            return (grouped[:].rearrange("p (c i) t -> p c t i", i=4), plain[:].rearrange("p t (c i) -> p c t i", i=4))
+            return (grouped.rearrange("p (c i) t -> p c t i", i=4), plain.rearrange("p t (c i) -> p c t i", i=4))
+
+        def cols(c):
+            return slice(c * CHUNK, (c + 1) * CHUNK)
 
         def group_hid(c):
-            dst, src = by_line(hid_grouped[c], hid[c])
+            dst, src = by_line(hid_grouped[c][:], part(hid, slice(0, PACK), c * CHUNK, (c + 1) * CHUNK))
             factor = unit_t[:].unsqueeze(1).to_broadcast(list(src.shape))
             nc.vector.tensor_tensor(dst, src, factor, ALU.mult)
 
-        def last_product(c):
-            lo, hi = CHUNKS[c]
-            n = hi - lo
-            cols = slice(lo, hi)
-            nc.vector.quantize_mx(h_codes[:, cols].bitcast(FP8X4), h_scales[:, cols], hid_grouped[c][:].rearrange("p n t -> p (n t)"))
-            per_bank = 2
-            for b in range(PACK // per_bank):
-                acc = psum.tile([P, per_bank, n], F32, name="out_acc%d_%d" % (c, b), tag="bank%d" % ((2 * c + b) % 4))
-                for u in range(per_bank):
-                    product(acc[:, u, :], w3_codes, w3_scales, per_bank * b + u, h_codes[:, cols], h_scales[:, cols])
-                (on_v if c == 2 and b == 1 else on_s)(result[c][:, per_bank * b : per_bank * (b + 1), :], acc[:])
-            nc.sync.dma_start(out_rows[:, :, cols], result[c][:])
+        def quantize_hid(c):
+            quantize(h_codes[:, cols(c)], h_scales[:, cols(c)], hid_grouped[c][:].rearrange("p n t -> p (n t)"))
 
-        out_grouped = [sb([P, hi - lo, PACK], BF16, "out_grouped%d" % c) for c, (lo, hi) in enumerate(CHUNKS)]
+        def last_product(c):
+            acc = psum.tile([P, PACK, CHUNK], F32, name="out_acc%d" % c, tag="bank%d" % c)
+            for t in range(PACK):
+                product(acc[:, t, :], w3_codes, w3_scales, t, h_codes[:, cols(c)], h_scales[:, cols(c)])
+            nc.scalar.copy(result[c][:], acc[:])
+            nc.sync.dma_start(out_rows[:, :, cols(c)], result[c][:])
 
         def group_planes(c, copy):
-            copy(*by_line(out_grouped[c], result[c]))
+            copy(*by_line(out_grouped[c][:], result[c][:]))
 
         def make_planes(c):
-            cols = slice(*CHUNKS[c])
-            nc.vector.quantize_mx(o_codes[:, cols].bitcast(FP8X4), o_scales[:, cols], out_grouped[c][:].rearrange("p n t -> p (n t)"))
-            nc.sync.dma_start(out_words[:, cols], o_codes[:, cols].bitcast(I32))
+            quantize(o_codes[:, cols(c)], o_scales[:, cols(c)], out_grouped[c][:].rearrange("p n t -> p (n t)"))
 
+        def store_words(lo, hi):
+            nc.sync.dma_start(out_words[:, lo:hi], o_codes[:, lo:hi].bitcast(I32))
+
+        every = slice(0, PACK)
         for t in range(PACK):
             make_em(t)
-        deal(scalar_copy, w3_grouped, w3_raw, 0, P)
+        gap.append(sb([P, PACK, HALF], F32, "gap1"))
         make_res1(0)
         make_res1(1)
-        fused_gap(0, 0)
-        fused_gap(1, 0)
+        fused_gap(0, 0, 256)
+        fused_gap(1, 0, 256)
         make_res1(2)
-        make_hid(0, 0)
-        make_hid(1, 0)
+        make_hid(0, 0, 256)
+        make_hid(1, 0, 256)
         make_res1(3)
-        fused_gap(2, 0)
-        fused_gap(3, 0)
+        fused_gap(2, 0, 256)
+        fetch_rp(3, 0, 256)
         for t in range(PACK):
-            fetch_rp(t, 1)
-        make_hid(2, 0)
-        make_hid(3, 0)
+            fetch_rp(t, 256, 384)
+        round_w3(on_s, 0, P)
+        late = sb([P, 2, PACK, CHUNK], F32, "late", tag="w3_raw")
+        last_gap, scaled = late[:, 0], late[:, 1]
         for t in range(PACK):
-            fetch_rp(t, 2)
-        nc.vector.quantize_mx(w3_codes[:].bitcast(FP8X4), w3_scales[:], w3_grouped[:])
+            fetch_rp(t, 384, 512)
+        make_hid(2, 0, 256)
+        plain_gap(3, 0, 256)
+        plain_gap(every, 256, 384)
+        make_hid(3, 0, 256)
+        make_hid(0, 256, 384)
         group_hid(0)
-        plain_gap(1, slice(0, 4))
+        for t in range(1, PACK):
+            make_hid(t, 256, 384)
+        quantize_hid(0)
+        quantize(w3_codes[:], w3_scales[:], w3_grouped[:])
+        hid_grouped[2] = sb([P, CHUNK, PACK], BF16, "hid_grouped_third", tag="w3_grouped")
         last_product(0)
-        make_hid(0, 1)
-        make_hid(1, 1)
-        make_hid(2, 1)
-        make_hid(3, 1)
-        group_planes(0, on_s)
-        plain_gap(2, slice(0, 4))
-        group_hid(1)
-        make_hid(0, 2)
-        make_hid(1, 2)
-        last_product(1)
-        group_planes(1, on_s)
-        make_hid(2, 2)
-        make_hid(3, 2)
-        make_planes(0)
+        for t in range(PACK):
+            nc.scalar.activation(scaled[:, t, :], part(hid, t, 128, 256), COPY, scale=unit_t[:, t, :])
+        on_s(*by_line(hid_grouped[1][:], scaled))
         group_hid(2)
+        plain_gap(every, 384, 512)
+        quantize_hid(2)
         last_product(2)
-        make_planes(1)
+        for t in range(PACK):
+            make_hid(t, 384, 512)
+        quantize_hid(1)
+        last_product(1)
+        group_hid(3)
+        group_planes(0, on_v)
+        quantize_hid(3)
+        last_product(3)
         group_planes(2, on_v)
+        make_planes(0)
+        group_planes(1, on_v)
         make_planes(2)
+        make_planes(1)
+        store_words(0, 384)
+        group_planes(3, on_v)
+        make_planes(3)
+        store_words(384, 512)
         for q in range(4):
             queue = nc.sync if q % 2 else nc.scalar
             queue.dma_start(out_2[0, 4 * q : 4 * q + 4, :].bitcast(I32), o_scales[32 * q : 32 * q + 4, :].bitcast(I32))

@@ -147,11 +147,13 @@ def tile_picked_ytransc_max_po_kernel(
                 return last_gap[:, ts, :]
             return tiles[lo // HALF][:, ts, lo % HALF : lo % HALF + hi - lo]
 
-        def make_em(t):
-            ye = sb([P, S], F32, "ye%d" % t)
-            nc.scalar.copy(ye[:], ye_acc[t][:])
+        ye = [sb([P, S], F32, "ye%d" % t) for t in range(PACK)]
+
+        def make_em(t, skip):
+            nc.scalar.copy(ye[t][:], ye_acc[t][:])
             for h in range(2):
-                nc.scalar.activation(em[:, t, h * HALF : (h + 1) * HALF], ye[:].indirect(md_t[:, h * 16 : (h + 1) * 16]), COPY)
+                if (t, h) not in skip:
+                    nc.scalar.activation(em[:, t, h * HALF : (h + 1) * HALF], ye[t][:].indirect(md_t[:, h * 16 : (h + 1) * 16]), COPY)
 
         def round_w3(copy, lo, hi):
             dst = w3_grouped[:].rearrange("p (t m j) -> p m t j", t=PACK, j=PACK)[:, lo:hi]
@@ -199,6 +201,14 @@ def tile_picked_ytransc_max_po_kernel(
             nc.scalar.copy(result[c][:], acc[:])
             nc.sync.dma_start(out_rows[:, :, cols(c)], result[c][:])
 
+        def split_last_product(c):
+            for b, copy in enumerate((on_s, on_v)):
+                acc = psum.tile([P, 2, CHUNK], F32, name="out_acc%d_%d" % (c, b), tag="bank%d" % (c * (1 - b)))
+                for u in range(2):
+                    product(acc[:, u, :], w3_codes, w3_scales, 2 * b + u, h_codes[:, cols(c)], h_scales[:, cols(c)])
+                copy(result[c][:, 2 * b : 2 * b + 2, :], acc[:])
+            nc.sync.dma_start(out_rows[:, :, cols(c)], result[c][:])
+
         def group_planes(c, copy):
             copy(*by_line(out_grouped[c][:], result[c][:]))
 
@@ -210,10 +220,12 @@ def tile_picked_ytransc_max_po_kernel(
 
         every = slice(0, PACK)
         for t in range(PACK):
-            make_em(t)
+            make_em(t, ())
         gap.append(sb([P, PACK, HALF], F32, "gap1"))
         make_res1(0)
         make_res1(1)
+        for t, h in ():
+            on_v(em[:, t, h * HALF : (h + 1) * HALF], ye[t][:].indirect(md_t[:, h * 16 : (h + 1) * 16]))
         fused_gap(0, 0, 256)
         fused_gap(1, 0, 256)
         make_res1(2)
@@ -221,7 +233,7 @@ def tile_picked_ytransc_max_po_kernel(
         make_hid(1, 0, 256)
         make_res1(3)
         fused_gap(2, 0, 256)
-        fetch_rp(3, 0, 256)
+        fused_gap(3, 0, 256)
         for t in range(PACK):
             fetch_rp(t, 256, 384)
         round_w3(on_s, 0, P)
@@ -230,7 +242,6 @@ def tile_picked_ytransc_max_po_kernel(
         for t in range(PACK):
             fetch_rp(t, 384, 512)
         make_hid(2, 0, 256)
-        plain_gap(3, 0, 256)
         plain_gap(every, 256, 384)
         make_hid(3, 0, 256)
         make_hid(0, 256, 384)
@@ -255,7 +266,7 @@ def tile_picked_ytransc_max_po_kernel(
         group_hid(3)
         group_planes(0, on_v)
         quantize_hid(3)
-        last_product(3)
+        split_last_product(3)
         group_planes(2, on_v)
         make_planes(0)
         group_planes(1, on_v)

from contextlib import ExitStack

import concourse.mybir as mybir

T, S, N = 1024, 512, 512
FLOPS = 3 * 2 * 512 * 512 * 512

F32 = mybir.dt.float32
BF16 = mybir.dt.bfloat16
I32 = mybir.dt.int32
U32 = mybir.dt.uint32
U16 = mybir.dt.uint16
U8 = mybir.dt.uint8
FP8X4 = mybir.dt.float8_e4m3fn_x4
ALU = mybir.AluOpType
COPY = mybir.ActivationFunctionType.Copy

P = 128
PACK = 4
HALF = 256
CHUNK = 128


def tile_picked_ytransc_max_po_kernel(
    tc, x_words, x_scales, w1, e_words, e_scales, w2, unit, w3, offs, mds, md, prv, out_0, out_1, out_2
):
    nc = tc.nc
    with ExitStack() as ctx:
        lists = ctx.enter_context(tc.tile_pool(name="lists", bufs=1))
        keep = ctx.enter_context(tc.tile_pool(name="keep", bufs=1))
        psum = ctx.enter_context(tc.psum_pool(name="psum", bufs=1))
        on_v, on_s = nc.vector.tensor_copy, nc.scalar.copy

        def on_g(dst, src):
            nc.gpsimd.tensor_scalar(dst, src, 1.0, 0.0, ALU.mult, ALU.add)

        def sb(shape, dtype, name, tag=""):
            return keep.tile(shape, dtype, name=name, tag=tag or name, align_bytes=64)

        def load_list(src, name):
            tile = lists.tile([P, S // 16], U16, name=name)
            nc.sync.dma_start(tile[:], src)
            return tile

        def load_scale_table(src, name):
            tile = sb([P, T], U8, name)
            nc.gpsimd.memset(tile[:].bitcast(I32), 0)
            for q in range(4):
                nc.sync.dma_start(tile[32 * q : 32 * q + 4, :].bitcast(I32), src[0, 4 * q : 4 * q + 4, :].bitcast(I32))
            return tile

        def load_word_table(src, name):
            tile = sb([P, T], I32, name)
            nc.sync.dma_start(tile[:], src[0].rearrange("p n t -> p (n t)").bitcast(I32))
            return tile

        def load_weight(w, name):
            tile = sb([P, PACK, N], F32, name)
            nc.sync.dma_start(tile[:], w.rearrange("(p j) c -> p j c", j=PACK))
            return tile

        def load_hidden_rows(src, width, name):
            tile = sb([P, PACK, width], F32, name)
            rows = src.rearrange("(c t r) n -> r c t n", t=PACK, r=4)
            for r in range(4):
                nc.sync.dma_start(tile[r:P:4], rows[r])
            return tile

        def round_tile(copy, grouped, raw, t, order="p t c j r"):
            dst = grouped[:].rearrange("p (t c r j) -> " + order, t=PACK, r=4, j=PACK)[:, t]
            copy(dst, raw[:].rearrange("p j (c t r) -> " + order, t=PACK, r=4)[:, t])

        def quantize(codes, scales, grouped):
            nc.vector.quantize_mx(codes.bitcast(FP8X4), scales, grouped)

        def quantize_tile(codes, scales, grouped, t):
            cols = slice(t * P, (t + 1) * P)
            quantize(codes[:, cols], scales[:, cols], grouped[:, t * 512 : (t + 1) * 512])

        def product(acc, w_codes, w_scales, t, codes, scales):
            cols = slice(t * P, (t + 1) * P)
            nc.tensor.matmul_mx(acc, lhsT=w_codes[:, cols].bitcast(FP8X4), lhsT_scale=w_scales[:, cols],
                                rhs=codes.bitcast(FP8X4), rhs_scale=scales, start=True, stop=True)

        mds_t = load_list(mds, "mds_t")
        e_word_table = load_word_table(e_words, "e_word_table")
        offs_t = load_list(offs, "offs_t")
        e_scale_table = load_scale_table(e_scales, "e_scale_table")
        w2_raw = load_weight(w2, "w2_raw")
        x_word_table = load_word_table(x_words, "x_word_table")
        md_t = load_list(md, "md_t")
        x_scale_table = load_scale_table(x_scales, "x_scale_table")
        w1_raw = load_weight(w1, "w1_raw")
        prv_t = load_list(prv, "prv_t")
        with nc.allow_non_contiguous_dma(reason="one factor for each hidden row"):
            unit_t = load_hidden_rows(unit, 1, "unit_t")
        w3_raw = load_hidden_rows(w3, N, "w3_raw")

        e_codes = sb([P, S], U32, "e_codes")
        e_bytes = sb([P, S], U8, "e_bytes")
        nc.vector.tensor_copy(e_codes[:], e_word_table[:].bitcast(U32).indirect(mds_t[:]))
        nc.vector.tensor_copy(e_bytes[:], e_scale_table[:].indirect(mds_t[:]))
        w2_grouped = sb([P, PACK * N], BF16, "w2_grouped")
        w2_codes = sb([P, N], U32, "w2_codes")
        w2_scales = sb([P, N], U8, "w2_scales")
        ye_acc = [psum.tile([P, S], F32, name="ye_acc%d" % t, tag="bank%d" % t) for t in range(PACK)]
        for t in range(PACK):
            round_tile(on_s if t % 2 else on_v, w2_grouped, w2_raw, t)
        for t in range(PACK):
            quantize_tile(w2_codes, w2_scales, w2_grouped, t)
            product(ye_acc[t][:], w2_codes, w2_scales, t, e_codes[:], e_bytes[:])

        x_codes = sb([P, S], U32, "x_codes")
        x_bytes = sb([P, S], U8, "x_bytes")
        w1_grouped = sb([P, PACK * N], BF16, "w1_grouped")
        w1_codes = sb([P, N], U32, "w1_codes")
        w1_scales = sb([P, N], U8, "w1_scales")
        y_acc = [psum.tile([P, S], F32, name="y_acc%d" % t) for t in range(PACK)]
        nc.vector.tensor_copy(x_codes[:], x_word_table[:].bitcast(U32).indirect(offs_t[:]))
        nc.vector.tensor_copy(x_bytes[:], x_scale_table[:].indirect(offs_t[:]))
        for t in range(PACK + 1):
            if t < PACK:
                round_tile(on_v, w1_grouped, w1_raw, t)
            if t:
                quantize_tile(w1_codes, w1_scales, w1_grouped, t - 1)
                product(y_acc[t - 1][:], w1_codes, w1_scales, t - 1, x_codes[:], x_bytes[:])

        em = sb([P, PACK, S], F32, "em")
        res1 = [sb([P, S], F32, "res1_%d" % t) for t in range(PACK)]
        gap = [sb([P, PACK, HALF], F32, "gap0")]
        hid = [sb([P, PACK, HALF], F32, "hid%d" % h) for h in range(2)]
        hid_grouped = [sb([P, CHUNK, PACK], BF16, "hid_grouped%d" % c) for c in range(4)]
        h_codes = sb([P, S], U32, "h_codes")
        h_scales = sb([P, S], U8, "h_scales")
        result = [sb([P, PACK, CHUNK], F32, "result%d" % c) for c in range(4)]
        out_grouped = [sb([P, CHUNK, PACK], BF16, "out_grouped%d" % c) for c in range(4)]
        w3_grouped = sb([P, PACK * N], BF16, "w3_grouped")
        w3_codes = sb([P, N], U32, "w3_codes")
        w3_scales = sb([P, N], U8, "w3_scales")
        o_codes = sb([P, S], U32, "o_codes")
        o_scales = sb([P, S], U8, "o_scales")
        out_rows = out_0.rearrange("(p t) n -> p t n", t=PACK)
        out_words = out_1[0].rearrange("p n t -> p (n t)").bitcast(I32)

        def part(tiles, ts, lo, hi):
            if tiles is gap and lo >= 384:
                return last_gap[:, ts, :]
            return tiles[lo // HALF][:, ts, lo % HALF : lo % HALF + hi - lo]

        ye = [sb([P, S], F32, "ye%d" % t) for t in range(PACK)]

        def make_em(t, skip):
            nc.scalar.copy(ye[t][:], ye_acc[t][:])
            for h in range(2):
                if (t, h) not in skip:
                    nc.scalar.activation(em[:, t, h * HALF : (h + 1) * HALF], ye[t][:].indirect(md_t[:, h * 16 : (h + 1) * 16]), COPY)

        def round_w3(copy, lo, hi):
            dst = w3_grouped[:].rearrange("p (t m j) -> p m t j", t=PACK, j=PACK)[:, lo:hi]
            copy(dst, w3_raw[:].rearrange("p j (m t) -> p m t j", t=PACK)[:, lo:hi])

        def make_res1(t):
            nc.vector.tensor_tensor(res1[t][:], y_acc[t][:], em[:, t, :], ALU.add)

        def looked_up(t, lo, hi):
            return res1[t][:].indirect(prv_t[:, lo // 16 : hi // 16])

        def fused_gap(t, lo, hi):
            nc.vector.tensor_tensor(part(gap, t, lo, hi), looked_up(t, lo, hi), em[:, t, lo:hi], ALU.subtract)

        def fetch_rp(t, lo, hi):
            nc.scalar.activation(part(gap, t, lo, hi), looked_up(t, lo, hi), COPY)

        def fetch_rp_v(t, lo, hi):
            nc.vector.tensor_copy(part(gap, t, lo, hi), looked_up(t, lo, hi))

        def plain_gap(ts, lo, hi):
            nc.vector.tensor_tensor(part(gap, ts, lo, hi), part(gap, ts, lo, hi), em[:, ts, lo:hi], ALU.subtract)

        def make_hid(t, lo, hi):
            nc.vector.scalar_tensor_tensor(part(hid, t, lo, hi), part(gap, t, lo, hi), 0.0, y_acc[t][:, lo:hi], ALU.max, ALU.subtract)

        def by_line(grouped, plain):
            return (grouped.rearrange("p (c i) t -> p c t i", i=4), plain.rearrange("p t (c i) -> p c t i", i=4))

        def cols(c):
            return slice(c * CHUNK, (c + 1) * CHUNK)

        def group_hid(c):
            dst, src = by_line(hid_grouped[c][:], part(hid, slice(0, PACK), c * CHUNK, (c + 1) * CHUNK))
            factor = unit_t[:].unsqueeze(1).to_broadcast(list(src.shape))
            nc.vector.tensor_tensor(dst, src, factor, ALU.mult)

        def quantize_hid(c):
            quantize(h_codes[:, cols(c)], h_scales[:, cols(c)], hid_grouped[c][:].rearrange("p n t -> p (n t)"))

        def last_product(c):
            acc = psum.tile([P, PACK, CHUNK], F32, name="out_acc%d" % c, tag="bank%d" % c)
            for t in range(PACK):
                product(acc[:, t, :], w3_codes, w3_scales, t, h_codes[:, cols(c)], h_scales[:, cols(c)])
            nc.scalar.copy(result[c][:], acc[:])
            nc.sync.dma_start(out_rows[:, :, cols(c)], result[c][:])

        def split_last_product(c):
            for b, copy in enumerate((on_s, on_v)):
                acc = psum.tile([P, 2, CHUNK], F32, name="out_acc%d_%d" % (c, b), tag="bank%d" % (c * (1 - b)))
                for u in range(2):
                    product(acc[:, u, :], w3_codes, w3_scales, 2 * b + u, h_codes[:, cols(c)], h_scales[:, cols(c)])
                copy(result[c][:, 2 * b : 2 * b + 2, :], acc[:])
            nc.sync.dma_start(out_rows[:, :, cols(c)], result[c][:])

        def group_planes(c, copy):
            copy(*by_line(out_grouped[c][:], result[c][:]))

        def make_planes(c):
            quantize(o_codes[:, cols(c)], o_scales[:, cols(c)], out_grouped[c][:].rearrange("p n t -> p (n t)"))

        def store_words(lo, hi):
            nc.sync.dma_start(out_words[:, lo:hi], o_codes[:, lo:hi].bitcast(I32))

        every = slice(0, PACK)
        for t in range(PACK):
            make_em(t, ())
        gap.append(sb([P, PACK, HALF], F32, "gap1"))
        make_res1(0)
        make_res1(1)
        for t, h in ():
            on_v(em[:, t, h * HALF : (h + 1) * HALF], ye[t][:].indirect(md_t[:, h * 16 : (h + 1) * 16]))
        fused_gap(0, 0, 256)
        fused_gap(1, 0, 256)
        make_res1(2)
        make_hid(0, 0, 256)
        make_hid(1, 0, 256)
        make_res1(3)
        fused_gap(2, 0, 256)
        fused_gap(3, 0, 256)
        for t in range(PACK):
            fetch_rp(t, 256, 384)
        round_w3(on_s, 0, P)
        late = sb([P, 2, PACK, CHUNK], F32, "late", tag="w3_raw")
        last_gap, scaled = late[:, 0], late[:, 1]
        for t in range(PACK):
            fetch_rp(t, 384, 512)
        make_hid(2, 0, 256)
        plain_gap(every, 256, 384)
        make_hid(3, 0, 256)
        make_hid(0, 256, 384)
        group_hid(0)
        for t in range(1, PACK):
            make_hid(t, 256, 384)
        quantize_hid(0)
        quantize(w3_codes[:], w3_scales[:], w3_grouped[:])
        hid_grouped[2] = sb([P, CHUNK, PACK], BF16, "hid_grouped_third", tag="w3_grouped")
        last_product(0)
        for t in range(PACK):
            nc.scalar.activation(scaled[:, t, :], part(hid, t, 128, 256), COPY, scale=unit_t[:, t, :])
        on_s(*by_line(hid_grouped[1][:], scaled))
        group_hid(2)
        plain_gap(every, 384, 512)
        quantize_hid(2)
        last_product(2)
        for t in range(PACK):
            make_hid(t, 384, 512)
        quantize_hid(1)
        last_product(1)
        group_hid(3)
        group_planes(0, on_v)
        quantize_hid(3)
        split_last_product(3)
        group_planes(2, on_v)
        make_planes(0)
        group_planes(1, on_v)
        make_planes(2)
        make_planes(1)
        store_words(0, 384)
        group_planes(3, on_v)
        make_planes(3)
        store_words(384, 512)
        for q in range(4):
            queue = nc.sync if q % 2 else nc.scalar
            queue.dma_start(out_2[0, 4 * q : 4 * q + 4, :].bitcast(I32), o_scales[32 * q : 32 * q + 4, :].bitcast(I32))
